import numpy as np
import ml_dtypes


def mxq(x, axis, fmt="e4m3"):
    dtype, down = {"e4m3": (ml_dtypes.float8_e4m3fn, 7), "e5m2": (ml_dtypes.float8_e5m2, 14)}[fmt]
    v = np.moveaxis(np.asarray(x, np.float32).astype(ml_dtypes.bfloat16).astype(np.float64), axis, -1)
    blocks = v.reshape(v.shape[:-1] + (-1, 32))
    amax = np.abs(blocks).max(-1, keepdims=True)
    byte = np.maximum(np.where(amax > 0, np.frexp(amax)[1] - 1 + 127, 0) - down, 1)
    scale = np.exp2(byte - 127.0)
    codes = (blocks / scale).astype(np.float32).astype(dtype).astype(np.float64)
    return np.moveaxis((codes * scale).reshape(v.shape), -1, axis)


WIDE = False


def mx_kscale(k):
    if not WIDE:
        return np.ones(k)
    levels = np.array([10, -10, 5, -5, 0])
    if k % 512:
        return np.exp2(np.random.permutation(np.resize(levels, k // 32))).repeat(32)
    a = np.empty((k // 512, 16))
    for p in range(k // 512):
        a[p, :8] = np.random.permutation(np.resize(levels, 8))
        for g in range(8):
            far = levels[np.abs(levels - a[p, g]) >= 10]
            a[p, g + 8] = far[np.random.randint(len(far))]
    return np.exp2(a.ravel()).repeat(32)


def f64(x):
    return np.asarray(x).astype(np.float64)


def striped(idx):
    return np.tile(idx.reshape(-1, 16).T, (8, 1)).astype(np.uint16)


def unstriped(offs):
    return offs[:16].T.reshape(-1).astype(np.int64)


def striped8(idx):
    return np.concatenate([x.reshape(-1, 16).T for x in idx]).astype(np.uint16)


def runs(offs, k):
    lists = np.stack([offs[16 * r : 16 * r + 16].T.reshape(-1) for r in range(8)]).astype(np.int64)
    return lists[np.arange(k) % 512 // 64]


def pack_weight(w):
    k, n = w.shape
    w = f64(np.asarray(w, np.float32).astype(ml_dtypes.bfloat16)).reshape(k // 32, 32, n)
    amax = np.abs(w).max(1)
    byte = np.clip(np.where(amax > 0, np.frexp(amax)[1] - 1 + 127 - 7, 1), 1, 254)
    scaled = (w * np.exp2(127.0 - byte)[:, None, :]).reshape(k, n).astype(np.float32)
    words = np.ascontiguousarray(scaled.reshape(k // 512, 128, 4, n).transpose(0, 1, 3, 2)).astype(ml_dtypes.float8_e4m3fn).view(np.uint8)
    return words, np.ascontiguousarray(byte.astype(np.uint8).reshape(k // 512, 16, n))


def unpack_weight(words, scales):
    g, p, n, _ = words.shape
    vals = np.ascontiguousarray(words).view(ml_dtypes.float8_e4m3fn).astype(np.float64) * np.repeat(np.exp2(scales.astype(np.float64) - 127.0), 8, axis=1)[..., None]
    return vals.transpose(0, 1, 3, 2).reshape(g * 512, n)


def sigmoid(v):
    return 1.0 / (1.0 + np.exp(-np.maximum(v, -700.0)))

def planes(y):
    n, m = y.shape
    v = y.astype(np.float32).astype(ml_dtypes.bfloat16).astype(np.float64).reshape(n // 32, 32, m)
    top = np.abs(v).max(1)
    byte = np.clip(np.where(top > 0, np.frexp(top)[1] - 1 + 127 - 7, 1), 1, 254)
    codes = (v * np.exp2(127.0 - byte)[:, None, :]).reshape(n, m).astype(np.float32).astype(ml_dtypes.float8_e4m3fn).view(np.uint8)
    words = codes.reshape(n // 512, 128, 4, m).transpose(0, 1, 3, 2)
    return np.ascontiguousarray(words), np.ascontiguousarray(byte.astype(np.uint8).reshape(n // 512, 16, m))


K, T, S, G, H, W = 512, 1024, 256, 2048, 512, 128


def setup_inputs():
    n = np.random.standard_normal
    s = mx_kscale(K)[:, None]
    packed_xT = pack_weight(n((K, T)) * s)
    packed_dT = pack_weight(n((K, G)) / s)
    perm = np.random.permutation(S)
    return {
        "x_words": packed_xT[0],
        "x_scales": packed_xT[1],
        "d_words": packed_dT[0],
        "d_scales": packed_dT[1],
        "gs": (np.random.uniform(0.5, 1.5, (K, 1)) * s).astype(np.float32),
        "sl": np.random.uniform(1.0, 2.0, (H, 1)).astype(np.float32),
        "th": (0.5 * n((H, 1))).astype(np.float32),
        "offs": striped8(np.random.randint(0, T, (8, S))),
        "k1": striped8(np.random.randint(0, G, (8, H))),
        "n1": striped(perm[:W]),
        "n2": striped(perm[W:]),
        "n3": striped(np.random.permutation(S)),
        "k2": striped8(np.random.randint(0, G, (8, H))),
        "n4": striped(np.random.permutation(S)),
        "n5": striped(np.random.permutation(S)),
    }


def reference(x_words, x_scales, d_words, d_scales, gs, sl, th, offs, k1, n1, n2, n3, k2, n4, n5):
    d_k2 = unpack_weight(d_words, d_scales)[np.arange(K)[:, None], runs(k2, K)]
    d_k1 = unpack_weight(d_words, d_scales)[np.arange(K)[:, None], runs(k1, K)]
    xq = unpack_weight(x_words, x_scales)[np.arange(K)[:, None], runs(offs, K)]
    h = 0.0625 * (d_k1.T @ xq)
    pa = h[:, unstriped(n1)]
    pb = h[:, unstriped(n2)]
    rb = pa - pb
    ds = np.zeros((H, S))
    ds[:, unstriped(n1)] = pb
    dt = ds.copy()
    dt[:, unstriped(n2)] = rb
    z = f64(gs) * (np.maximum(dt, 0.5 * dt[:, unstriped(n3)]))
    h2 = 0.0625 * ((d_k2.T @ mxq(z, 0, "e4m3")))
    ds2 = np.zeros((H, S))
    ds2[:, unstriped(n4)] = h2
    sg = sigmoid(f64(sl) * (ds2[:, unstriped(n5)] - f64(th)))
    out_0 = h2 * sg
    return (out_0,) + planes(out_0)

@@ -1,0 +1,244 @@
+from contextlib import ExitStack
+
+import concourse.mybir as mybir
+
+F32 = mybir.dt.float32
+BF16 = mybir.dt.bfloat16
+I32 = mybir.dt.int32
+U32 = mybir.dt.uint32
+U16 = mybir.dt.uint16
+U8 = mybir.dt.uint8
+FP8X4 = mybir.dt.float8_e4m3fn_x4
+ALU = mybir.AluOpType
+ACT = mybir.ActivationFunctionType
+
+P = 128
+PACK = 4
+K, T, S, G, H = 512, 1024, 256, 2048, 512
+HALF = S // 2
+LIST_COLS = HALF // 16
+FLOPS = 2 * 2 * K * H * S
+
+
+def tile_picked_hcodeswapderl_none_po_kernel(
+    tc, x_words, x_scales, d_words, d_scales, gs, sl, th, offs, k1, n1, n2, n3, k2, n4, n5, out_0, out_1, out_2
+):
+    nc = tc.nc
+    tiles = range(PACK)
+    halves = range(2)
+
+    with ExitStack() as ctx:
+        keep = ctx.enter_context(tc.tile_pool(name="keep", bufs=1))
+        psum = ctx.enter_context(tc.psum_pool(name="psum", bufs=2))
+
+        def sb(name, width, dtype, tag=None):
+            made = keep.tile([P, width], dtype, name=name, tag=tag or name, align_bytes=64)
+            return made
+
+        def load_list(name, src):
+            lst = keep.tile(list(src.shape), U16, name=name)
+            nc.sync.dma_start(lst[:], src)
+            return lst
+
+        def load_scale_rows(name, src, width):
+            table = sb(name, width, U8)
+            rows = src[0].bitcast(I32).unsqueeze(1).to_broadcast([16, 8, width // 4])
+            nc.sync.dma_start(table[:].bitcast(I32), rows)
+            return table
+
+        def load_words(name, src, width):
+            table = sb(name, width, I32)
+            nc.sync.dma_start(table[:], src[0].rearrange("p n t -> p (n t)").bitcast(I32))
+            return table
+
+        def load_row_values(name, src):
+            vals = sb(name, PACK, F32)
+            nc.gpsimd.dma_start(vals[:], src.rearrange("(p t) o -> p (t o)", t=PACK))
+            return vals
+
+        k1_l = load_list("k1_l", k1)
+        d_bytes = load_scale_rows("d_bytes", d_scales, G)
+        offs_l = load_list("offs_l", offs)
+        x_bytes = load_scale_rows("x_bytes", x_scales, T)
+        n2_l = load_list("n2_l", n2)
+        n1_l = load_list("n1_l", n1)
+        d_tab = load_words("d_tab", d_words, G)
+        x_tab = load_words("x_tab", x_words, T)
+        k2_l = load_list("k2_l", k2)
+        n3_l = load_list("n3_l", n3)
+        n4_l = load_list("n4_l", n4)
+        n5_l = load_list("n5_l", n5)
+        gs_t = load_row_values("gs_t", gs)
+        sl_t = load_row_values("sl_t", sl)
+        th_t = load_row_values("th_t", th)
+        neg_th = sb("neg_th", PACK, F32)
+        nc.gpsimd.tensor_scalar(neg_th[:], th_t[:], -1.0, 0.0, ALU.mult, ALU.add)
+        neg_bias = sb("neg_bias", PACK, F32)
+        nc.gpsimd.tensor_tensor(neg_bias[:], sl_t[:], neg_th[:], ALU.mult)
+
+        def place_scale_rows(name, picked, width, queue):
+            placed = sb(name, width, U8)
+            nc.vector.tensor_copy(placed[:].bitcast(I32), picked[:].bitcast(I32))
+            for j in range(1, 4):
+                queue.dma_start(placed[j:P:32, :].bitcast(I32), picked[8 * j : P : 32, :].bitcast(I32))
+            return placed
+
+        def deal(name, picked, t, dtype):
+            dealt = sb(name, P, dtype)
+            nc.vector.tensor_copy(dealt[:], picked[:, t:H:PACK])
+            return dealt
+
+        bytes1 = sb("bytes1", H + S, U8)
+        nc.vector.tensor_copy(bytes1[:, 0:H], d_bytes[:].indirect(k1_l[:]))
+        nc.vector.tensor_copy(bytes1[:, H : H + S], x_bytes[:].indirect(offs_l[:]))
+        placed1 = place_scale_rows("placed1", bytes1, H + S, nc.scalar)
+        w1 = sb("w1", H, U32)
+        nc.vector.tensor_copy(w1[:], d_tab[:].bitcast(U32).indirect(k1_l[:]))
+        w1_t = [deal("w1_0", w1, 0, U32)]
+        xw = sb("xw", S, U32)
+        nc.vector.tensor_copy(xw[:], x_tab[:].bitcast(U32).indirect(offs_l[:]))
+
+        h = []
+        for t in tiles:
+            if t > 0:
+                w1_t.append(deal("w1_%d" % t, w1, t, U32))
+            s1 = deal("s1_%d" % t, placed1, t, U8)
+            acc = psum.tile([P, S], F32, name="acc", tag="acc%d" % t)
+            nc.tensor.matmul_mx(
+                out=acc[:], lhsT=w1_t[t][:].bitcast(FP8X4), lhsT_scale=s1[:],
+                rhs=xw[:].bitcast(FP8X4), rhs_scale=placed1[:, H : H + S], start=True, stop=True,
+            )
+            h_t = sb("h_%d" % t, S, F32)
+            nc.vector.tensor_scalar(h_t[:], acc[:], 0.0625, None, ALU.mult)
+            h.append(h_t)
+
+        pa = [sb("pa_%d" % t, HALF, F32)[:] for t in tiles]
+        pb = [sb("pb_%d" % t, HALF, F32)[:] for t in tiles]
+        shared = sb("shared", S, F32)
+        rb = [sb("rb_%d" % t, HALF, F32)[:] for t in range(PACK - 1)] + [shared[:, HALF // 2 : HALF // 2 + HALF]]
+        far = {(t, 0): sb("far_%d_0" % t, HALF, F32)[:] for t in tiles}
+        far[(0, 1)] = pb[3]
+        far[(1, 1)] = shared[:, 0:HALF]
+        far[(2, 1)] = shared[:, HALF:S]
+        far[(3, 1)] = sb("far_3_1", HALF, F32)[:]
+        dt = [sb("dt_%d" % t, S, F32) for t in tiles]
+        z_bf = [keep.tile([P, HALF, PACK], BF16, name="z_bf_%d" % u, align_bytes=64) for u in halves]
+
+        def fetch_pairs(t):
+            nc.scalar.activation(pb[t], h[t][:].indirect(n2_l[:]), ACT.Copy)
+            nc.scalar.activation(pa[t], h[t][:].indirect(n1_l[:]), ACT.Copy)
+            nc.vector.tensor_tensor(rb[t], pa[t], pb[t], ALU.subtract)
+
+        def put_pb(t):
+            nc.scalar.activation(dt[t][:].indirect(n1_l[:]), pb[t], ACT.Copy)
+
+        def put_rb(t):
+            nc.scalar.activation(dt[t][:].indirect(n2_l[:]), rb[t], ACT.Copy)
+
+        def half_list(lst, u):
+            return lst[:, u * LIST_COLS : (u + 1) * LIST_COLS]
+
+        def make_z(t, u):
+            nc.scalar.activation(far[(t, u)], dt[t][:].indirect(half_list(n3_l, u)), ACT.Copy)
+            top = sb("top_%d_%d" % (t, u), HALF, F32)
+            nc.vector.scalar_tensor_tensor(top[:], far[(t, u)], 0.5, dt[t][:, u * HALF : (u + 1) * HALF], ALU.mult, ALU.max)
+            nc.vector.tensor_scalar(z_bf[u][:, :, t], top[:], gs_t[:, t : t + 1], None, ALU.mult)
+
+        fetch_pairs(0)
+        put_pb(0)
+        fetch_pairs(1)
+
+        bytes2 = sb("bytes2", H, U8, tag="placed1")
+        w2 = sb("w2", H, U32, tag="xw")
+        for u in halves:
+            cols = slice(u * H // 2, (u + 1) * H // 2)
+            nc.vector.tensor_copy(bytes2[:, cols], d_bytes[:].indirect(k2_l[:, u * 16 : (u + 1) * 16]))
+        placed2 = place_scale_rows("placed2", bytes2, H, nc.sync)
+
+        put_rb(0)
+        put_pb(1)
+        fetch_pairs(2)
+        for u in halves:
+            cols = slice(u * H // 2, (u + 1) * H // 2)
+            nc.vector.tensor_copy(w2[:, cols], d_tab[:].bitcast(U32).indirect(k2_l[:, u * 16 : (u + 1) * 16]))
+        make_z(0, 0)
+        put_rb(1)
+        put_pb(2)
+        fetch_pairs(3)
+        w2_t = [deal("w2_%d" % t, w2, t, U32) for t in tiles]
+        s2_t = [deal("s2_%d" % t, placed2, t, U8) for t in tiles]
+        make_z(1, 0)
+        put_rb(2)
+        put_pb(3)
+        make_z(2, 0)
+        put_rb(3)
+        make_z(0, 1)
+        make_z(3, 0)
+
+        h2 = [[None, None] for t in tiles]
+
+        def second_layer(u):
+            zw = sb("zw_%d" % u, HALF, U32)
+            zs = sb("zs_%d" % u, HALF, U8)
+            nc.vector.quantize_mx(out=zw[:].bitcast(FP8X4), scales=zs[:], in_=z_bf[u][:].rearrange("p c t -> p (c t)"))
+            for t in tiles:
+                acc = psum.tile([P, S], F32, name="acc", tag="acc%d" % t)
+                nc.tensor.matmul_mx(
+                    out=acc[:, 0:HALF], lhsT=w2_t[t][:].bitcast(FP8X4), lhsT_scale=s2_t[t][:],
+                    rhs=zw[:].bitcast(FP8X4), rhs_scale=zs[:], start=True, stop=True,
+                )
+                h2[t][u] = sb("h2_%d_%d" % (t, u), HALF, F32)
+                nc.vector.tensor_scalar(h2[t][u][:], acc[:, 0:HALF], 0.0625, None, ALU.mult)
+
+        second_layer(0)
+        for t in range(1, PACK):
+            make_z(t, 1)
+        second_layer(1)
+
+        ds2 = [sb("ds2_%d" % t, S, F32) for t in tiles]
+        res = [keep.tile([P, PACK, HALF], F32, name="res_%d" % u, align_bytes=64) for u in halves]
+        res_bf = [keep.tile([P, HALF, PACK], BF16, name="res_bf_%d" % u, align_bytes=64) for u in halves]
+        out_w = [sb("out_w_%d" % u, HALF, I32) for u in halves]
+        out_s = sb("out_s", S, U8)
+        out_rows = out_0.rearrange("(p t) c -> p t c", t=PACK)
+        out_words = out_1[0].rearrange("p n t -> p (n t)").bitcast(I32)
+
+        def put_h2(t, u):
+            nc.scalar.activation(ds2[t][:].indirect(half_list(n4_l, u)), h2[t][u][:], ACT.Copy)
+
+        def finish(t, u):
+            cols = slice(u * HALF, (u + 1) * HALF)
+            sg = sb("sg_%d_%d" % (t, u), HALF, F32)
+            nc.scalar.activation(
+                sg[:], ds2[t][:].indirect(half_list(n5_l, u)), ACT.Sigmoid,
+                bias=neg_bias[:, t : t + 1], scale=sl_t[:, t : t + 1],
+            )
+            nc.vector.tensor_tensor(res[u][:, t, :], h2[t][u][:], sg[:], ALU.mult)
+            nc.sync.dma_start(out_rows[:, t, cols], res[u][:, t, :])
+            if t % 2 == 1:
+                nc.vector.tensor_copy(
+                    res_bf[u][:, :, t - 1 : t + 1], res[u][:, t - 1 : t + 1, :].rearrange("p t c -> p c t")
+                )
+            if t == PACK - 1:
+                nc.vector.quantize_mx(
+                    out=out_w[u][:].bitcast(FP8X4), scales=out_s[:, cols], in_=res_bf[u][:].rearrange("p c t -> p (c t)")
+                )
+                nc.sync.dma_start(out_words[:, cols], out_w[u][:])
+
+        for t in tiles:
+            put_h2(t, 0)
+        put_h2(0, 1)
+        put_h2(1, 1)
+        finish(0, 0)
+        put_h2(2, 1)
+        finish(1, 0)
+        finish(0, 1)
+        finish(2, 0)
+        put_h2(3, 1)
+        finish(1, 1)
+        finish(3, 0)
+        finish(2, 1)
+        finish(3, 1)
+        for q in range(4):
+            queue = nc.scalar if q % 2 else nc.sync
+            queue.dma_start(out_2[0][4 * q : 4 * q + 4, :].bitcast(I32), out_s[32 * q : 32 * q + 4, :].bitcast(I32))

@@ -56,18 +56,22 @@ def tile_picked_hcodeswapderl_none_po_kernel(
             nc.gpsimd.dma_start(vals[:], src.rearrange("(p t) o -> p (t o)", t=PACK))
             return vals
 
-        k1_l = load_list("k1_l", k1)
-        d_bytes = load_scale_rows("d_bytes", d_scales, G)
         offs_l = load_list("offs_l", offs)
         x_bytes = load_scale_rows("x_bytes", x_scales, T)
-        n2_l = load_list("n2_l", n2)
-        n1_l = load_list("n1_l", n1)
+        k1_l = load_list("k1_l", k1)
+        d_bytes = load_scale_rows("d_bytes", d_scales, G)
         d_tab = load_words("d_tab", d_words, G)
         x_tab = load_words("x_tab", x_words, T)
+        n2_l = load_list("n2_l", n2)
+        n1_l = load_list("n1_l", n1)
         k2_l = load_list("k2_l", k2)
         n3_l = load_list("n3_l", n3)
         n4_l = load_list("n4_l", n4)
         n5_l = load_list("n5_l", n5)
+        warm_in = sb("warm_in", 8, F32)
+        nc.vector.memset(warm_in[:], 0.0)
+        warm_out = sb("warm_out", 8, F32)
+        nc.scalar.activation(warm_out[:], warm_in[:], ACT.Sigmoid)
         gs_t = load_row_values("gs_t", gs)
         sl_t = load_row_values("sl_t", sl)
         th_t = load_row_values("th_t", th)
@@ -89,8 +93,8 @@ def tile_picked_hcodeswapderl_none_po_kernel(
             return dealt
 
         bytes1 = sb("bytes1", H + S, U8)
-        nc.vector.tensor_copy(bytes1[:, 0:H], d_bytes[:].indirect(k1_l[:]))
         nc.vector.tensor_copy(bytes1[:, H : H + S], x_bytes[:].indirect(offs_l[:]))
+        nc.vector.tensor_copy(bytes1[:, 0:H], d_bytes[:].indirect(k1_l[:]))
         placed1 = place_scale_rows("placed1", bytes1, H + S, nc.scalar)
         w1 = sb("w1", H, U32)
         nc.vector.tensor_copy(w1[:], d_tab[:].bitcast(U32).indirect(k1_l[:]))
@@ -99,13 +103,15 @@ def tile_picked_hcodeswapderl_none_po_kernel(
         nc.vector.tensor_copy(xw[:], x_tab[:].bitcast(U32).indirect(offs_l[:]))
 
         h = []
+        s1_all = sb("s1_all", H, U8, tag="x_tab")
         for t in tiles:
             if t > 0:
                 w1_t.append(deal("w1_%d" % t, w1, t, U32))
-            s1 = deal("s1_%d" % t, placed1, t, U8)
+            s1 = s1_all[:, t * P : (t + 1) * P]
+            nc.vector.tensor_copy(s1, placed1[:, t:H:PACK])
             acc = psum.tile([P, S], F32, name="acc", tag="acc%d" % t)
             nc.tensor.matmul_mx(
-                out=acc[:], lhsT=w1_t[t][:].bitcast(FP8X4), lhsT_scale=s1[:],
+                out=acc[:], lhsT=w1_t[t][:].bitcast(FP8X4), lhsT_scale=s1,
                 rhs=xw[:].bitcast(FP8X4), rhs_scale=placed1[:, H : H + S], start=True, stop=True,
             )
             h_t = sb("h_%d" % t, S, F32)
@@ -114,12 +120,10 @@ def tile_picked_hcodeswapderl_none_po_kernel(
 
         pa = [sb("pa_%d" % t, HALF, F32)[:] for t in tiles]
         pb = [sb("pb_%d" % t, HALF, F32)[:] for t in tiles]
-        shared = sb("shared", S, F32)
-        rb = [sb("rb_%d" % t, HALF, F32)[:] for t in range(PACK - 1)] + [shared[:, HALF // 2 : HALF // 2 + HALF]]
-        far = {(t, 0): sb("far_%d_0" % t, HALF, F32)[:] for t in tiles}
-        far[(0, 1)] = pb[3]
-        far[(1, 1)] = shared[:, 0:HALF]
-        far[(2, 1)] = shared[:, HALF:S]
+        rb = [sb("rb_%d" % t, HALF, F32)[:] for t in range(PACK - 1)]
+        far = {(t, 0): sb("far_%d_0" % t, HALF, F32)[:] for t in (0, 1, 3)}
+        far[(2, 0)] = pb[3]
+        far[(0, 1)] = pa[3]
         far[(3, 1)] = sb("far_3_1", HALF, F32)[:]
         dt = [sb("dt_%d" % t, S, F32) for t in tiles]
         z_bf = [keep.tile([P, HALF, PACK], BF16, name="z_bf_%d" % u, align_bytes=64) for u in halves]
@@ -138,11 +142,12 @@ def tile_picked_hcodeswapderl_none_po_kernel(
         def half_list(lst, u):
             return lst[:, u * LIST_COLS : (u + 1) * LIST_COLS]
 
-        def make_z(t, u):
+        def fetch_far(t, u):
             nc.scalar.activation(far[(t, u)], dt[t][:].indirect(half_list(n3_l, u)), ACT.Copy)
-            top = sb("top_%d_%d" % (t, u), HALF, F32)
-            nc.vector.scalar_tensor_tensor(top[:], far[(t, u)], 0.5, dt[t][:, u * HALF : (u + 1) * HALF], ALU.mult, ALU.max)
-            nc.vector.tensor_scalar(z_bf[u][:, :, t], top[:], gs_t[:, t : t + 1], None, ALU.mult)
+
+        def make_z(t, u, top):
+            nc.vector.scalar_tensor_tensor(top, far[(t, u)], 0.5, dt[t][:, u * HALF : (u + 1) * HALF], ALU.mult, ALU.max)
+            nc.vector.tensor_scalar(z_bf[u][:, :, t], top, gs_t[:, t : t + 1], None, ALU.mult)
 
         fetch_pairs(0)
         put_pb(0)
@@ -161,21 +166,32 @@ def tile_picked_hcodeswapderl_none_po_kernel(
         for u in halves:
             cols = slice(u * H // 2, (u + 1) * H // 2)
             nc.vector.tensor_copy(w2[:, cols], d_tab[:].bitcast(U32).indirect(k2_l[:, u * 16 : (u + 1) * 16]))
-        make_z(0, 0)
+        fetch_far(0, 0)
         put_rb(1)
         put_pb(2)
+        w2_all = sb("w2_all", H, U32)
+        nc.vector.tensor_copy(w2_all[:].rearrange("p (t m) -> p t m", t=PACK), w2[:].rearrange("p (m t) -> p t m", t=PACK))
+        s2_all = sb("s2_all", H, U8)
+        nc.vector.tensor_copy(s2_all[:].rearrange("p (t m) -> p t m", t=PACK), placed2[:].rearrange("p (m t) -> p t m", t=PACK))
+        shared = sb("shared", S, F32)
+        tops = sb("tops", PACK * HALF, F32, tag="placed2")
+        top_a = [tops[:, t * HALF : (t + 1) * HALF] for t in tiles]
+        rb.append(shared[:, HALF // 2 : HALF // 2 + HALF])
+        far[(1, 1)] = shared[:, 0:HALF]
+        far[(2, 1)] = shared[:, HALF:S]
         fetch_pairs(3)
-        w2_t = [deal("w2_%d" % t, w2, t, U32) for t in tiles]
-        s2_t = [deal("s2_%d" % t, placed2, t, U8) for t in tiles]
-        make_z(1, 0)
         put_rb(2)
         put_pb(3)
-        make_z(2, 0)
+        fetch_far(1, 0)
         put_rb(3)
-        make_z(0, 1)
-        make_z(3, 0)
+        fetch_far(2, 0)
+        fetch_far(3, 0)
+        for t in tiles:
+            make_z(t, 0, top_a[t])
+        for t in tiles:
+            fetch_far(t, 1)
 
-        h2 = [[None, None] for t in tiles]
+        h2 = [sb("h2_%d" % t, S, F32) for t in tiles]
 
         def second_layer(u):
             zw = sb("zw_%d" % u, HALF, U32)
@@ -184,61 +200,67 @@ def tile_picked_hcodeswapderl_none_po_kernel(
             for t in tiles:
                 acc = psum.tile([P, S], F32, name="acc", tag="acc%d" % t)
                 nc.tensor.matmul_mx(
-                    out=acc[:, 0:HALF], lhsT=w2_t[t][:].bitcast(FP8X4), lhsT_scale=s2_t[t][:],
+                    out=acc[:, 0:HALF], lhsT=w2_all[:, t * P : (t + 1) * P].bitcast(FP8X4), lhsT_scale=s2_all[:, t * P : (t + 1) * P],
                     rhs=zw[:].bitcast(FP8X4), rhs_scale=zs[:], start=True, stop=True,
                 )
-                h2[t][u] = sb("h2_%d_%d" % (t, u), HALF, F32)
-                nc.vector.tensor_scalar(h2[t][u][:], acc[:, 0:HALF], 0.0625, None, ALU.mult)
+                nc.vector.tensor_scalar(h2[t][:, u * HALF : (u + 1) * HALF], acc[:, 0:HALF], 0.0625, None, ALU.mult)
 
         second_layer(0)
-        for t in range(1, PACK):
-            make_z(t, 1)
+        top_b = sb("top_b", PACK * HALF, F32, tag="z_bf_0")
+        for t in tiles:
+            make_z(t, 1, top_b[:, t * HALF : (t + 1) * HALF])
         second_layer(1)
 
-        ds2 = [sb("ds2_%d" % t, S, F32) for t in tiles]
-        res = [keep.tile([P, PACK, HALF], F32, name="res_%d" % u, align_bytes=64) for u in halves]
-        res_bf = [keep.tile([P, HALF, PACK], BF16, name="res_bf_%d" % u, align_bytes=64) for u in halves]
-        out_w = [sb("out_w_%d" % u, HALF, I32) for u in halves]
+        ds2 = [sb("ds2_%d" % t, 2 * S, F32) for t in tiles]
+        res = [keep.tile([P, 2, S], F32, name="res_%d" % pair, align_bytes=64) for pair in range(2)]
+        res_bf = keep.tile([P, S, PACK], BF16, name="res_bf", align_bytes=64)
+        out_w = sb("out_w", S, I32)
         out_s = sb("out_s", S, U8)
         out_rows = out_0.rearrange("(p t) c -> p t c", t=PACK)
         out_words = out_1[0].rearrange("p n t -> p (n t)").bitcast(I32)
 
         def put_h2(t, u):
-            nc.scalar.activation(ds2[t][:].indirect(half_list(n4_l, u)), h2[t][u][:], ACT.Copy)
+            nc.scalar.activation(ds2[t][:].indirect(half_list(n4_l, u)), h2[t][:, u * HALF : (u + 1) * HALF], ACT.Copy)
 
-        def finish(t, u):
-            cols = slice(u * HALF, (u + 1) * HALF)
-            sg = sb("sg_%d_%d" % (t, u), HALF, F32)
+        def gate(t, lo, hi):
+            sg = sb("sg_%d_%d" % (t, lo), hi - lo, F32)
             nc.scalar.activation(
-                sg[:], ds2[t][:].indirect(half_list(n5_l, u)), ACT.Sigmoid,
+                sg[:], ds2[t][:].indirect(n5_l[:, lo // 16 : hi // 16]), ACT.Sigmoid,
                 bias=neg_bias[:, t : t + 1], scale=sl_t[:, t : t + 1],
             )
-            nc.vector.tensor_tensor(res[u][:, t, :], h2[t][u][:], sg[:], ALU.mult)
-            nc.sync.dma_start(out_rows[:, t, cols], res[u][:, t, :])
-            if t % 2 == 1:
-                nc.vector.tensor_copy(
-                    res_bf[u][:, :, t - 1 : t + 1], res[u][:, t - 1 : t + 1, :].rearrange("p t c -> p c t")
-                )
-            if t == PACK - 1:
-                nc.vector.quantize_mx(
-                    out=out_w[u][:].bitcast(FP8X4), scales=out_s[:, cols], in_=res_bf[u][:].rearrange("p c t -> p (c t)")
-                )
-                nc.sync.dma_start(out_words[:, cols], out_w[u][:])
+            nc.vector.tensor_tensor(res[t // 2][:, t % 2, lo:hi], h2[t][:, lo:hi], sg[:], ALU.mult)
+
+        def round_pair(pair, lo, hi):
+            nc.vector.tensor_copy(
+                res_bf[:, lo:hi, 2 * pair : 2 * pair + 2], res[pair][:, :, lo:hi].rearrange("p t c -> p c t")
+            )
+
+        def planes(lo, hi):
+            nc.vector.quantize_mx(
+                out=out_w[:, lo:hi].bitcast(FP8X4), scales=out_s[:, lo:hi],
+                in_=res_bf[:, lo:hi, :].rearrange("p c t -> p (c t)"),
+            )
+            nc.sync.dma_start(out_words[:, lo:hi], out_w[:, lo:hi])
 
         for t in tiles:
             put_h2(t, 0)
         put_h2(0, 1)
         put_h2(1, 1)
-        finish(0, 0)
+        gate(0, 0, S)
         put_h2(2, 1)
-        finish(1, 0)
-        finish(0, 1)
-        finish(2, 0)
+        gate(1, 0, S)
+        nc.sync.dma_start(out_rows[:, 0:2, :], res[0][:])
+        round_pair(0, 0, S)
         put_h2(3, 1)
-        finish(1, 1)
-        finish(3, 0)
-        finish(2, 1)
-        finish(3, 1)
+        gate(2, 0, S)
+        nc.sync.dma_start(out_rows[:, 2, :], res[1][:, 0, :])
+        gate(3, 0, HALF)
+        gate(3, HALF, S)
+        nc.scalar.dma_start(out_rows[:, 3, :], res[1][:, 1, :])
+        round_pair(1, 0, HALF)
+        round_pair(1, HALF, S)
+        planes(0, HALF)
+        planes(HALF, S)
         for q in range(4):
-            queue = nc.scalar if q % 2 else nc.sync
+            queue = nc.sync if q % 2 else nc.scalar
             queue.dma_start(out_2[0][4 * q : 4 * q + 4, :].bitcast(I32), out_s[32 * q : 32 * q + 4, :].bitcast(I32))

@@ -29,6 +29,7 @@ def tile_picked_hcodeswapderl_none_po_kernel(
 
     with ExitStack() as ctx:
         keep = ctx.enter_context(tc.tile_pool(name="keep", bufs=1))
+        reuse = ctx.enter_context(tc.tile_pool(name="reuse", bufs=1))
         psum = ctx.enter_context(tc.psum_pool(name="psum", bufs=2))
 
         def sb(name, width, dtype, tag=None):
@@ -46,8 +47,7 @@ def tile_picked_hcodeswapderl_none_po_kernel(
             nc.sync.dma_start(table[:].bitcast(I32), rows)
             return table
 
-        def load_words(name, src, width):
-            table = sb(name, width, I32)
+        def load_words(table, src):
             nc.sync.dma_start(table[:], src[0].rearrange("p n t -> p (n t)").bitcast(I32))
             return table
 
@@ -60,11 +60,11 @@ def tile_picked_hcodeswapderl_none_po_kernel(
         x_bytes = load_scale_rows("x_bytes", x_scales, T)
         k1_l = load_list("k1_l", k1)
         d_bytes = load_scale_rows("d_bytes", d_scales, G)
-        d_tab = load_words("d_tab", d_words, G)
-        x_tab = load_words("x_tab", x_words, T)
         n2_l = load_list("n2_l", n2)
         n1_l = load_list("n1_l", n1)
         k2_l = load_list("k2_l", k2)
+        d_tab = load_words(sb("d_tab", G, I32), d_words)
+        x_tab = load_words(reuse.tile([P, T], I32, name="x_tab", offset=0, align_bytes=64), x_words)
         n3_l = load_list("n3_l", n3)
         n4_l = load_list("n4_l", n4)
         n5_l = load_list("n5_l", n5)
@@ -87,8 +87,7 @@ def tile_picked_hcodeswapderl_none_po_kernel(
                 queue.dma_start(placed[j:P:32, :].bitcast(I32), picked[8 * j : P : 32, :].bitcast(I32))
             return placed
 
-        def deal(name, picked, t, dtype):
-            dealt = sb(name, P, dtype)
+        def deal(dealt, picked, t):
             nc.vector.tensor_copy(dealt[:], picked[:, t:H:PACK])
             return dealt
 
@@ -98,20 +97,18 @@ def tile_picked_hcodeswapderl_none_po_kernel(
         placed1 = place_scale_rows("placed1", bytes1, H + S, nc.scalar)
         w1 = sb("w1", H, U32)
         nc.vector.tensor_copy(w1[:], d_tab[:].bitcast(U32).indirect(k1_l[:]))
-        w1_t = [deal("w1_0", w1, 0, U32)]
+        w1_t = [deal(sb("w1_0", P, U32), w1, 0)]
         xw = sb("xw", S, U32)
         nc.vector.tensor_copy(xw[:], x_tab[:].bitcast(U32).indirect(offs_l[:]))
 
         h = []
-        s1_all = sb("s1_all", H, U8, tag="x_tab")
         for t in tiles:
             if t > 0:
-                w1_t.append(deal("w1_%d" % t, w1, t, U32))
-            s1 = s1_all[:, t * P : (t + 1) * P]
-            nc.vector.tensor_copy(s1, placed1[:, t:H:PACK])
+                w1_t.append(deal(reuse.tile([P, P], U32, name="w1_%d" % t, offset=1024 * t, align_bytes=64), w1, t))
+            s1 = deal(reuse.tile([P, P], U8, name="s1_%d" % t, offset=1024 * t + 512, align_bytes=64), placed1, t)
             acc = psum.tile([P, S], F32, name="acc", tag="acc%d" % t)
             nc.tensor.matmul_mx(
-                out=acc[:], lhsT=w1_t[t][:].bitcast(FP8X4), lhsT_scale=s1,
+                out=acc[:], lhsT=w1_t[t][:].bitcast(FP8X4), lhsT_scale=s1[:],
                 rhs=xw[:].bitcast(FP8X4), rhs_scale=placed1[:, H : H + S], start=True, stop=True,
             )
             h_t = sb("h_%d" % t, S, F32)

from contextlib import ExitStack

import concourse.mybir as mybir

F32 = mybir.dt.float32
BF16 = mybir.dt.bfloat16
I32 = mybir.dt.int32
U32 = mybir.dt.uint32
U16 = mybir.dt.uint16
U8 = mybir.dt.uint8
FP8X4 = mybir.dt.float8_e4m3fn_x4
ALU = mybir.AluOpType
ACT = mybir.ActivationFunctionType

P = 128
PACK = 4
K, T, S, G, H = 512, 1024, 256, 2048, 512
HALF = S // 2
LIST_COLS = HALF // 16
FLOPS = 2 * 2 * K * H * S


def tile_picked_hcodeswapderl_none_po_kernel(
    tc, x_words, x_scales, d_words, d_scales, gs, sl, th, offs, k1, n1, n2, n3, k2, n4, n5, out_0, out_1, out_2
):
    nc = tc.nc
    tiles = range(PACK)
    halves = range(2)

    with ExitStack() as ctx:
        keep = ctx.enter_context(tc.tile_pool(name="keep", bufs=1))
        reuse = ctx.enter_context(tc.tile_pool(name="reuse", bufs=1))
        psum = ctx.enter_context(tc.psum_pool(name="psum", bufs=2))

        def sb(name, width, dtype, tag=None):
            made = keep.tile([P, width], dtype, name=name, tag=tag or name, align_bytes=64)
            return made

        def load_list(name, src):
            lst = keep.tile(list(src.shape), U16, name=name)
            nc.sync.dma_start(lst[:], src)
            return lst

        def load_scale_rows(name, src, width):
            table = sb(name, width, U8)
            rows = src[0].bitcast(I32).unsqueeze(1).to_broadcast([16, 8, width // 4])
            nc.sync.dma_start(table[:].bitcast(I32), rows)
            return table

        def load_words(table, src):
            nc.sync.dma_start(table[:], src[0].rearrange("p n t -> p (n t)").bitcast(I32))
            return table

        def load_row_values(name, src):
            vals = sb(name, PACK, F32)
            nc.gpsimd.dma_start(vals[:], src.rearrange("(p t) o -> p (t o)", t=PACK))
            return vals

        offs_l = load_list("offs_l", offs)
        x_bytes = load_scale_rows("x_bytes", x_scales, T)
        k1_l = load_list("k1_l", k1)
        d_bytes = load_scale_rows("d_bytes", d_scales, G)
        n2_l = load_list("n2_l", n2)
        n1_l = load_list("n1_l", n1)
        k2_l = load_list("k2_l", k2)
        d_tab = load_words(sb("d_tab", G, I32), d_words)
        x_tab = load_words(reuse.tile([P, T], I32, name="x_tab", offset=0, align_bytes=64), x_words)
        n3_l = load_list("n3_l", n3)
        n4_l = load_list("n4_l", n4)
        n5_l = load_list("n5_l", n5)
        warm_in = sb("warm_in", 8, F32)
        nc.vector.memset(warm_in[:], 0.0)
        warm_out = sb("warm_out", 8, F32)
        nc.scalar.activation(warm_out[:], warm_in[:], ACT.Sigmoid)
        gs_t = load_row_values("gs_t", gs)
        sl_t = load_row_values("sl_t", sl)
        th_t = load_row_values("th_t", th)
        neg_th = sb("neg_th", PACK, F32)
        nc.gpsimd.tensor_scalar(neg_th[:], th_t[:], -1.0, 0.0, ALU.mult, ALU.add)
        neg_bias = sb("neg_bias", PACK, F32)
        nc.gpsimd.tensor_tensor(neg_bias[:], sl_t[:], neg_th[:], ALU.mult)

        def place_scale_rows(name, picked, width, queue):
            placed = sb(name, width, U8)
            nc.vector.tensor_copy(placed[:].bitcast(I32), picked[:].bitcast(I32))
            for j in range(1, 4):
                queue.dma_start(placed[j:P:32, :].bitcast(I32), picked[8 * j : P : 32, :].bitcast(I32))
            return placed

        def deal(dealt, picked, t):
            nc.vector.tensor_copy(dealt[:], picked[:, t:H:PACK])
            return dealt

        bytes1 = sb("bytes1", H + S, U8)
        nc.vector.tensor_copy(bytes1[:, H : H + S], x_bytes[:].indirect(offs_l[:]))
        nc.vector.tensor_copy(bytes1[:, 0:H], d_bytes[:].indirect(k1_l[:]))
        placed1 = place_scale_rows("placed1", bytes1, H + S, nc.scalar)
        w1 = sb("w1", H, U32)
        nc.vector.tensor_copy(w1[:], d_tab[:].bitcast(U32).indirect(k1_l[:]))
        w1_t = [deal(sb("w1_0", P, U32), w1, 0)]
        xw = sb("xw", S, U32)
        nc.vector.tensor_copy(xw[:], x_tab[:].bitcast(U32).indirect(offs_l[:]))

        h = []
        for t in tiles:
            if t > 0:
                w1_t.append(deal(reuse.tile([P, P], U32, name="w1_%d" % t, offset=1024 * t, align_bytes=64), w1, t))
            s1 = deal(reuse.tile([P, P], U8, name="s1_%d" % t, offset=1024 * t + 512, align_bytes=64), placed1, t)
            acc = psum.tile([P, S], F32, name="acc", tag="acc%d" % t)
            nc.tensor.matmul_mx(
                out=acc[:], lhsT=w1_t[t][:].bitcast(FP8X4), lhsT_scale=s1[:],
                rhs=xw[:].bitcast(FP8X4), rhs_scale=placed1[:, H : H + S], start=True, stop=True,
            )
            h_t = sb("h_%d" % t, S, F32)
            nc.vector.tensor_scalar(h_t[:], acc[:], 0.0625, None, ALU.mult)
            h.append(h_t)

        pa = [sb("pa_%d" % t, HALF, F32)[:] for t in tiles]
        pb = [sb("pb_%d" % t, HALF, F32)[:] for t in tiles]
        rb = [sb("rb_%d" % t, HALF, F32)[:] for t in range(PACK - 1)]
        far = {(t, 0): sb("far_%d_0" % t, HALF, F32)[:] for t in (0, 1, 3)}
        far[(2, 0)] = pb[3]
        far[(0, 1)] = pa[3]
        far[(3, 1)] = sb("far_3_1", HALF, F32)[:]
        dt = [sb("dt_%d" % t, S, F32) for t in tiles]
        z_bf = [keep.tile([P, HALF, PACK], BF16, name="z_bf_%d" % u, align_bytes=64) for u in halves]

        def fetch_pairs(t):
            nc.scalar.activation(pb[t], h[t][:].indirect(n2_l[:]), ACT.Copy)
            nc.scalar.activation(pa[t], h[t][:].indirect(n1_l[:]), ACT.Copy)
            nc.vector.tensor_tensor(rb[t], pa[t], pb[t], ALU.subtract)

        def put_pb(t):
            nc.scalar.activation(dt[t][:].indirect(n1_l[:]), pb[t], ACT.Copy)

        def put_rb(t):
            nc.scalar.activation(dt[t][:].indirect(n2_l[:]), rb[t], ACT.Copy)

        def half_list(lst, u):
            return lst[:, u * LIST_COLS : (u + 1) * LIST_COLS]

        def fetch_far(t, u):
            nc.scalar.activation(far[(t, u)], dt[t][:].indirect(half_list(n3_l, u)), ACT.Copy)

        def make_z(t, u, top):
            nc.vector.scalar_tensor_tensor(top, far[(t, u)], 0.5, dt[t][:, u * HALF : (u + 1) * HALF], ALU.mult, ALU.max)
            nc.vector.tensor_scalar(z_bf[u][:, :, t], top, gs_t[:, t : t + 1], None, ALU.mult)

        fetch_pairs(0)
        put_pb(0)
        fetch_pairs(1)

        bytes2 = sb("bytes2", H, U8, tag="placed1")
        w2 = sb("w2", H, U32, tag="xw")
        for u in halves:
            cols = slice(u * H // 2, (u + 1) * H // 2)
            nc.vector.tensor_copy(bytes2[:, cols], d_bytes[:].indirect(k2_l[:, u * 16 : (u + 1) * 16]))
        placed2 = place_scale_rows("placed2", bytes2, H, nc.sync)

        put_rb(0)
        put_pb(1)
        fetch_pairs(2)
        for u in halves:
            cols = slice(u * H // 2, (u + 1) * H // 2)
            nc.vector.tensor_copy(w2[:, cols], d_tab[:].bitcast(U32).indirect(k2_l[:, u * 16 : (u + 1) * 16]))
        fetch_far(0, 0)
        put_rb(1)
        put_pb(2)
        w2_all = sb("w2_all", H, U32)
        nc.vector.tensor_copy(w2_all[:].rearrange("p (t m) -> p t m", t=PACK), w2[:].rearrange("p (m t) -> p t m", t=PACK))
        s2_all = sb("s2_all", H, U8)
        nc.vector.tensor_copy(s2_all[:].rearrange("p (t m) -> p t m", t=PACK), placed2[:].rearrange("p (m t) -> p t m", t=PACK))
        shared = sb("shared", S, F32)
        tops = sb("tops", PACK * HALF, F32, tag="placed2")
        top_a = [tops[:, t * HALF : (t + 1) * HALF] for t in tiles]
        rb.append(shared[:, HALF // 2 : HALF // 2 + HALF])
        far[(1, 1)] = shared[:, 0:HALF]
        far[(2, 1)] = shared[:, HALF:S]
        fetch_pairs(3)
        put_rb(2)
        put_pb(3)
        fetch_far(1, 0)
        put_rb(3)
        fetch_far(2, 0)
        fetch_far(3, 0)
        for t in tiles:
            make_z(t, 0, top_a[t])
        for t in tiles:
            fetch_far(t, 1)

        h2 = [sb("h2_%d" % t, S, F32) for t in tiles]

        def second_layer(u):
            zw = sb("zw_%d" % u, HALF, U32)
            zs = sb("zs_%d" % u, HALF, U8)
            nc.vector.quantize_mx(out=zw[:].bitcast(FP8X4), scales=zs[:], in_=z_bf[u][:].rearrange("p c t -> p (c t)"))
            for t in tiles:
                acc = psum.tile([P, S], F32, name="acc", tag="acc%d" % t)
                nc.tensor.matmul_mx(
                    out=acc[:, 0:HALF], lhsT=w2_all[:, t * P : (t + 1) * P].bitcast(FP8X4), lhsT_scale=s2_all[:, t * P : (t + 1) * P],
                    rhs=zw[:].bitcast(FP8X4), rhs_scale=zs[:], start=True, stop=True,
                )
                nc.vector.tensor_scalar(h2[t][:, u * HALF : (u + 1) * HALF], acc[:, 0:HALF], 0.0625, None, ALU.mult)

        second_layer(0)
        top_b = sb("top_b", PACK * HALF, F32, tag="z_bf_0")
        for t in tiles:
            make_z(t, 1, top_b[:, t * HALF : (t + 1) * HALF])
        second_layer(1)

        ds2 = [sb("ds2_%d" % t, 2 * S, F32) for t in tiles]
        res = [keep.tile([P, 2, S], F32, name="res_%d" % pair, align_bytes=64) for pair in range(2)]
        res_bf = keep.tile([P, S, PACK], BF16, name="res_bf", align_bytes=64)
        out_w = sb("out_w", S, I32)
        out_s = sb("out_s", S, U8)
        out_rows = out_0.rearrange("(p t) c -> p t c", t=PACK)
        out_words = out_1[0].rearrange("p n t -> p (n t)").bitcast(I32)

        def put_h2(t, u):
            nc.scalar.activation(ds2[t][:].indirect(half_list(n4_l, u)), h2[t][:, u * HALF : (u + 1) * HALF], ACT.Copy)

        def gate(t, lo, hi):
            sg = sb("sg_%d_%d" % (t, lo), hi - lo, F32)
            nc.scalar.activation(
                sg[:], ds2[t][:].indirect(n5_l[:, lo // 16 : hi // 16]), ACT.Sigmoid,
                bias=neg_bias[:, t : t + 1], scale=sl_t[:, t : t + 1],
            )
            nc.vector.tensor_tensor(res[t // 2][:, t % 2, lo:hi], h2[t][:, lo:hi], sg[:], ALU.mult)

        def round_pair(pair, lo, hi):
            nc.vector.tensor_copy(
                res_bf[:, lo:hi, 2 * pair : 2 * pair + 2], res[pair][:, :, lo:hi].rearrange("p t c -> p c t")
            )

        def planes(lo, hi):
            nc.vector.quantize_mx(
                out=out_w[:, lo:hi].bitcast(FP8X4), scales=out_s[:, lo:hi],
                in_=res_bf[:, lo:hi, :].rearrange("p c t -> p (c t)"),
            )
            nc.sync.dma_start(out_words[:, lo:hi], out_w[:, lo:hi])

        for t in tiles:
            put_h2(t, 0)
        put_h2(0, 1)
        put_h2(1, 1)
        gate(0, 0, S)
        put_h2(2, 1)
        gate(1, 0, S)
        nc.sync.dma_start(out_rows[:, 0:2, :], res[0][:])
        round_pair(0, 0, S)
        put_h2(3, 1)
        gate(2, 0, S)
        nc.sync.dma_start(out_rows[:, 2, :], res[1][:, 0, :])
        gate(3, 0, HALF)
        gate(3, HALF, S)
        nc.scalar.dma_start(out_rows[:, 3, :], res[1][:, 1, :])
        round_pair(1, 0, HALF)
        round_pair(1, HALF, S)
        planes(0, HALF)
        planes(HALF, S)
        for q in range(4):
            queue = nc.sync if q % 2 else nc.scalar
            queue.dma_start(out_2[0][4 * q : 4 * q + 4, :].bitcast(I32), out_s[32 * q : 32 * q + 4, :].bitcast(I32))
